import numpy as np, ml_dtypes
CORES = [83,85,87,115,117,119]
N = 6
J, Q = 1024, 8192
def entries(a): return a.T.reshape(-1)
def pack(v, P): return np.ascontiguousarray(np.asarray(v, np.int32).reshape(-1, P).T)
def split(rng, total, parts):
    c = np.sort(rng.integers(0, total + 1, parts - 1)); return np.diff(np.concatenate([[0], c, [total]]))
def lists(rng, how):
    s = np.concatenate([[0], rng.integers(1 - Q // 2, Q // 2 + 1, N - 1), [int(rng.integers(1 - Q // 2, 1))]])
    if how == "early": s[1:] = -Q; s[N] = -2 * Q
    if how == "late": s[1:] = Q; s[N] = 0
    if how == "long":
        z = int(rng.integers(1, N - 1)); s[1:z] = -rng.integers(1, Q, z - 1); s[z] = -Q; s[z + 1] = Q; s[z + 2:N] = rng.integers(1, Q, N - z - 2); s[N] = -int(rng.integers(0, Q - s[N - 1] + 1))
    if how == "sway":
        z = int(rng.integers(1, N - 2)); e = int(rng.integers(z + 1, N - 1)); s[1:] = -rng.integers(Q // 2 + 1, Q, N); s[z + 1:e + 1] = rng.integers(Q // 2 + 1, Q - 1, e - z); s[e + 1] = s[e] - Q; s[N] = s[N - 1] - Q + int(rng.integers(1, -s[N - 1]))
    tot = Q + np.diff(s)
    L = np.stack([split(rng, int(t), J) for t in tot])
    if how == "gaps":
        L = np.zeros((N, J), np.int64)
        for r in range(N): m = 1 if r & 1 else 8; L[r, 1 + rng.permutation(J - 2)[:m]] = split(rng, int(tot[r]), m)
    if how == "long":
        L = np.zeros((N, J), np.int64); L[np.arange(N), rng.integers(0, J, N)] = tot
    return {"ln": np.stack([pack(l, 16) for l in L])}
def setup_inputs(rng):
    return dict({"x": rng.standard_normal((N, 128, J), dtype=np.float32).astype(ml_dtypes.bfloat16)}, **lists(rng, "uniform"))
def setup_inputs_early(rng):
    d = setup_inputs(rng); d.update(lists(rng, "early"))
    for k in ("x",): d[k] = (d[k].astype(np.float32) * 1048576.0).astype(d[k].dtype)
    return d
def setup_inputs_gaps(rng):
    d = setup_inputs(rng); d.update(lists(rng, "gaps"))
    for k in ("x",): d[k] = (d[k].astype(np.float32) * (1 / 1024.0)).astype(d[k].dtype)
    return d
def setup_inputs_late(rng):
    d = setup_inputs(rng); d.update(lists(rng, "late"))
    return d
def setup_inputs_long(rng):
    d = setup_inputs(rng); d.update(lists(rng, "long"))
    return d
def setup_inputs_sway(rng):
    d = setup_inputs(rng); d.update(lists(rng, "sway"))
    return d
def check_inputs(x):
    bad = []
    if x["ln"].min() < 0 or x["ln"].max() >= N * Q + 1: bad.append("ln out of range")
    if int(x["ln"].sum()) > N * Q: bad.append("the lengths come to more than N * Q")
    c = np.concatenate([[0], np.cumsum([int(a.sum()) for a in x["ln"]])])
    if any(c[r] < (r - 1) * Q or c[r + 1] > (r + 2) * Q for r in range(N)): bad.append("the sums of the lengths before or up to a rank leave their bounds")
    return bad
def reference(x, ln):
    got = np.concatenate([np.repeat(x[r], entries(ln[r]), axis=1) for r in range(N)], axis=1)[:, :N * Q]
    Y = np.zeros((128, N * Q), x.dtype); Y[:, :got.shape[1]] = got
    return {"y": np.stack([Y[:, Q * r:Q * r + Q] for r in range(N)])}

@@ -1,0 +1,249 @@
+from concourse.bass import DstId, RemoteDMATransfer
+from concourse.mybir import AluOpType, ActivationFunctionType
+
+ALU = AluOpType
+J, Q = 1024, 8192
+PITCH = 12
+NB = 65
+SGP = 72
+BATCH = 4
+MAGIC = 1.5 * 2.0 ** 30
+PIECES = [(512, "s"), (512, "v"), (1024, "s"), (1024, "v"), (1536, "s"), (1280, "v"), (1152, "s"), (1152, "v")]
+
+SCRATCH = {
+    "lnr": ("sbuf", [128, 64], "int32"),
+    "X": ("sbuf", [128, 64], "float32"),
+    "RH": ("sbuf", [128, 20], "float32"),
+    "TL": ("sbuf", [128, 128], "float32"),
+    "ones": ("sbuf", [128, 72], "float32"),
+    "neg": ("sbuf", [128, 8], "float32"),
+    "e127": ("sbuf", [128, 4], "float32"),
+    "f127": ("sbuf", [128, 4], "float32"),
+    "kc": ("sbuf", [128, 8], "float32"),
+    "rowr": ("sbuf", [128, 128], "bfloat16"),
+    "arow": ("sbuf", [128, 128], "bfloat16"),
+    "brow": ("sbuf", [128, SGP], "bfloat16"),
+    "SA": ("sbuf", [128, 1024], "bfloat16"),
+    "SB": ("sbuf", [128, 1024], "bfloat16"),
+    "C": ("sbuf", [128, 72], "float32"),
+    "Cc": ("sbuf", [128, 72], "float32"),
+    "M": ("sbuf", [128, 36], "float32"),
+    "FB": ("sbuf", [128, 36], "float32"),
+    "A": ("sbuf", [128, 36], "float32"),
+    "LE": ("sbuf", [128, 24 * 128], "bfloat16"),
+    "SG": ("sbuf", [128, 24 * SGP], "bfloat16"),
+    "W16": ("sbuf", [128, SGP], "float16"),
+    "off": ("sbuf", [128, 512], "uint16"),
+    "win": ("sbuf", [128, 3 * J + 16], "bfloat16"),
+    "yo": ("sbuf", [128, Q], "bfloat16"),
+    "psD": ("psum", [128, 512], "float32"),
+    "psW": ("psum", [128, 512], "float32"),
+    "psO": ("psum", [128, 512], "float32"),
+}
+SEMAPHORES = (["ln", "lx", "m1", "m2", "gr", "gs", "ga", "vc", "pd", "vd", "vf", "sab", "cin", "xin", "ls", "vq", "va",
+               "pw", "vw", "po", "ve0", "ve1", "st"]
+              + ["cv%d" % b for b in range(6)] + ["cs%d" % b for b in range(6)] + ["g%d" % i for i in range(len(PIECES))])
+
+
+def engines(mask):
+    return bin(mask).count("1")
+
+
+def plan(topo, src, on, off):
+    m_off = 0
+    for d in off:
+        m_off = topo.mask(src, d)
+    m_on = 0
+    for d in on:
+        m_on = topo.mask(src, d) & ~m_off
+    return m_on, m_off
+
+
+def split_dsts(topo, src, dsts):
+    on = [d for d in dsts if topo.chip(d) == topo.chip(src)]
+    return on, [d for d in dsts if d not in on]
+
+
+def c_dsts(cores, r):
+    return [cores[s] for s in range(len(cores)) if s != r and s >= r - 1]
+
+
+def x_dsts(cores, r):
+    return [cores[s] for s in (r - 1, r + 1) if 0 <= s < len(cores)]
+
+
+def count_in(topo, cores, r, dsts_of):
+    tot = 0
+    for k in range(len(cores)):
+        if k == r:
+            continue
+        dsts = dsts_of(cores, k)
+        if cores[r] not in dsts:
+            continue
+        on, off = split_dsts(topo, cores[k], dsts)
+        m_on, m_off = plan(topo, cores[k], on, off)
+        tot += engines(m_on if cores[r] in on else m_off)
+    return tot
+
+
+def send(g, topo, core, dsts, outs, src, remote_sem, local_sem):
+    on, off = split_dsts(topo, core, dsts)
+    m_on, m_off = plan(topo, core, on, off)
+    transfers, n = [], 0
+    for group, m in ((off, m_off), (on, m_on)):
+        if group:
+            ids = []
+            for d in group:
+                rid, pid, _ = topo.addr(d)
+                ids.append(DstId(rid=rid, pnc=pid))
+            transfers.append(RemoteDMATransfer(dst_ids=ids, dma_engine_mask=m, remote_sem=remote_sem,
+                                               srcs=[src], dsts=[outs[d] for d in group], alu_op=0))
+            n += engines(m)
+    g.remote_dma_fused(transfers, local_sem=local_sem)
+    return n
+
+
+def rank_program(g, core, T, topo):
+    r = T.rank_of(core)
+    if r is None:
+        return
+    cores = T.cores
+    n_ranks = len(cores)
+    lo, hi = max(r - 1, 0), min(r + 1, n_ranks - 1)
+    nl = hi - lo + 1
+    nent = nl * J
+    nch = nl * 8
+    S = T.sem
+    v, sc, sy, te = g.vector, g.scalar, g.sync, g.tensor
+    w0 = J * (lo - (r - 1))
+    tail = r >= n_ranks - 2
+    w1 = w0 + nent + (8 if tail else 0)
+
+    sy.dma_start(T.lnr[0:16, :], T.ln[:]).then_inc(S.ln, 16)
+    sc.dma_start(T.win[:, J:2 * J], T.x[:]).then_inc(S.lx, 16)
+
+    v.memset(T.ones[:], 1.0).then_inc(S.m1, 1)
+    v.memset(T.neg[:], -1.0).then_inc(S.m1, 1)
+    n2 = 0
+    for ap, val in ((T.X[0:32, :], 0.0), (T.TL[0:32, :], 0.0), (T.TL[32:48, :], 1.0),
+                    (T.RH[32:48, 0:18:9], 1.0), (T.RH[32:48, 1:8], 0.0), (T.RH[32:48, 10:17], 0.0), (T.RH[32:48, 8:18:9], -1.0),
+                    (T.C[:, PITCH * r + 10:PITCH * r + 12], 0.0)):
+        v.memset(ap, val).then_inc(S.m2, 1)
+        n2 += 1
+    if tail:
+        v.memset(T.win[:, w0 + nent:w1], 0.0).then_inc(S.m2, 1)
+        n2 += 1
+
+    g.wait_ge(S.m1, 2)
+    for h in range(2):
+        g.affine_select(T.RH[0:32, 9 * h + 1:9 * h + 8], T.ones[0:32, 0:7], [[-1, 7]], ALU.is_equal, 0.0, -8 * h - 1, 1).then_inc(S.gr, 1)
+    g.affine_select(T.RH[0:32, 0:18:9], T.neg[0:32, 0:2], [[-8, 2]], ALU.is_gt, 0.0, 0, 1).then_inc(S.gr, 1)
+    g.affine_select(T.RH[0:32, 8:18:9], T.ones[0:32, 0:2], [[-8, 2]], ALU.is_gt, 0.0, -7, 1).then_inc(S.gr, 1)
+    g.affine_select(T.e127[:, 0:1], T.ones[:, 0:1], [[0, 1]], ALU.is_equal, 0.0, -127, 1).then_inc(S.gs, 1)
+    g.iota(T.kc[:], [[-16, 8]], 0, 1, allow_small_or_imprecise_dtypes=True).then_inc(S.gs, 1)
+    g.iota(T.rowr[:], [[0, 8], [1, 16]], 0, 0, allow_small_or_imprecise_dtypes=True).then_inc(S.gs, 1)
+    g.iota(T.arow[:], [[1, 128]], 1, 0, allow_small_or_imprecise_dtypes=True).then_inc(S.ga, 1)
+    g.iota(T.brow[:, 0:NB], [[-128, NB]], 0, 0, allow_small_or_imprecise_dtypes=True).then_inc(S.ga, 1)
+
+    v.wait_ge(S.m1, 2)
+    v.wait_ge(S.m2, n2)
+    v.wait_ge(S.ln, 16)
+    v.tensor_copy(T.X[0:16, :], T.lnr[0:16, :]).then_inc(S.vc, 1)
+    v.wait_ge(S.vc, 1)
+    v.tensor_tensor_scan(T.X[32:48, :], T.ones[0:16, 0:64], T.X[0:16, :], 0.0, ALU.mult, ALU.add).then_inc(S.vc, 1)
+
+    te.wait_ge(S.m2, n2)
+    te.wait_ge(S.gr, 4)
+    te.wait_ge(S.vc, 2)
+    for h in range(2):
+        te.matmul(T.psD[64 * h:64 * h + 64, 0:9], T.X[0:48, :], T.RH[0:48, 9 * h:9 * h + 9], True, True).then_inc(S.pd, 1)
+    te.matmul(T.psD[:, 9:10], T.TL[0:48, :], T.X[0:48, 63:64], True, True).then_inc(S.pd, 1)
+
+    v.wait_ge(S.pd, 3)
+    v.tensor_copy(T.C[:, PITCH * r:PITCH * r + 10], T.psD[:, 0:10]).then_inc(S.vd, 1)
+
+    nls = 0
+    g.wait_ge(S.m2, n2)
+    g.wait_ge(S.vd, 1)
+    dsts = c_dsts(cores, r)
+    slot = T.C[:, PITCH * r:PITCH * r + PITCH]
+    nls += send(g, topo, core, dsts, {d: slot for d in dsts}, slot, S.cin, S.ls)
+    g.wait_ge(S.lx, 16)
+    dsts = x_dsts(cores, r)
+    outs = {}
+    for d in dsts:
+        a = J * (r - T.rank_of(d) + 1)
+        outs[d] = T.win[:, a:a + J]
+    nls += send(g, topo, core, dsts, outs, T.win[:, J:2 * J], S.xin, S.ls)
+
+    v.wait_ge(S.gs, 3)
+    v.tensor_scalar(T.f127[:, 0:1], T.e127[:, 0:1], 1.0, None, ALU.subtract).then_inc(S.vf, 1)
+    v.wait_ge(S.vf, 1)
+    for h in range(8):
+        v.tensor_scalar(T.SA[:, 128 * h:128 * h + 128], T.rowr[:], T.kc[:, h:h + 1], T.e127[:, 0:1], ALU.is_equal, ALU.add).then_inc(S.sab, 1)
+        v.tensor_scalar(T.SB[:, 128 * h:128 * h + 128], T.rowr[:], T.kc[:, h:h + 1], T.f127[:, 0:1], ALU.not_equal, ALU.add).then_inc(S.sab, 1)
+
+    ncol = PITCH * (hi + 1)
+    c0 = PITCH * lo
+    cw = ncol - c0
+    v.wait_ge(S.vd, 1)
+    v.wait_ge(S.cin, count_in(topo, cores, r, c_dsts))
+    v.tensor_tensor_scan(T.Cc[:, 0:ncol], T.ones[:, 0:ncol], T.C[:, 0:ncol], 0.5 - Q * r, ALU.mult, ALU.add).then_inc(S.vq, 1)
+    v.wait_ge(S.vq, 1)
+    v.tensor_scalar(T.M[:, 0:cw], T.Cc[:, c0:ncol], -64.0, MAGIC, ALU.add, ALU.add).then_inc(S.va, 1)
+    v.wait_ge(S.va, 1)
+    v.tensor_scalar(T.FB[:, 0:cw], T.M[:, 0:cw], MAGIC, None, ALU.subtract).then_inc(S.va, 1)
+    v.wait_ge(S.va, 2)
+    v.tensor_tensor(T.A[:, 0:cw], T.Cc[:, c0:ncol], T.FB[:, 0:cw], ALU.subtract).then_inc(S.va, 1)
+    v.wait_ge(S.va, 3)
+    v.wait_ge(S.ga, 2)
+    col = [PITCH * (k // 8) + k % 8 for k in range(nch)]
+    for k in range(nch):
+        v.tensor_scalar(T.LE[:, 128 * k:128 * k + 128], T.arow[:], T.A[:, col[k]:col[k] + 1], 0.5, ALU.is_ge, ALU.subtract).then_inc(S["cv%d" % (k // BATCH)], 1)
+    sc.wait_ge(S.ga, 2)
+    sc.wait_ge(S.vq, 1)
+    for k in range(nch):
+        sc.activation(T.SG[:, SGP * k:SGP * k + NB], T.brow[:, 0:NB], ActivationFunctionType.Sign,
+                      bias=T.Cc[:, c0 + col[k]:c0 + col[k] + 1]).then_inc(S["cs%d" % (k // BATCH)], 1)
+    for k in range(nch):
+        if k % BATCH == 0:
+            te.wait_ge(S["cv%d" % (k // BATCH)], BATCH)
+            te.wait_ge(S["cs%d" % (k // BATCH)], BATCH)
+        mm = te.matmul(T.psW[:, 0:NB], T.LE[:, 128 * k:128 * k + 128], T.SG[:, SGP * k:SGP * k + NB], k == 0, k == nch - 1)
+        if k == nch - 1:
+            mm.then_inc(S.pw, 1)
+
+    v.wait_ge(S.pw, 1)
+    v.tensor_copy(T.W16[:, 0:NB], T.psW[:, 0:NB]).then_inc(S.vw, 1)
+    te.wait_ge(S.sab, 16)
+    te.wait_ge(S.vw, 1)
+    for h in range(8):
+        te.matmul(T.psO[:, h:512:8], T.SA[:, 128 * h:128 * h + 128], T.W16[:, 1:NB], True, False)
+        te.matmul(T.psO[:, h:512:8], T.SB[:, 128 * h:128 * h + 128], T.W16[:, 0:NB - 1], False, True).then_inc(S.po, 1)
+    v.wait_ge(S.po, 8)
+    e0 = (PIECES[0][0] + PIECES[1][0]) // 16
+    v.tensor_scalar(T.off[:, 0:e0], T.psO[:, 0:e0], -0.5, nent / 2.0, ALU.mult, ALU.add).then_inc(S.ve0, 1)
+    v.tensor_scalar(T.off[:, e0:512], T.psO[:, e0:512], -0.5, nent / 2.0, ALU.mult, ALU.add).then_inc(S.ve1, 1)
+
+    nx = count_in(topo, cores, r, x_dsts)
+    for q in (v, sc):
+        q.wait_ge(S.xin, nx)
+        q.wait_ge(S.lx, 16)
+        q.wait_ge(S.ve0, 1)
+    sc.wait_ge(S.m2, n2)
+    waited = {"s": False, "v": False}
+    t = 0
+    for i, (n, who) in enumerate(PIECES):
+        if (t + n) // 16 > e0 and not waited[who]:
+            (v if who == "v" else sc).wait_ge(S.ve1, 1)
+            waited[who] = True
+        src = T.win[:, w0:w1].indirect(T.off[:, t // 16:(t + n) // 16])
+        if who == "v":
+            v.tensor_copy(T.yo[:, t:t + n], src).then_inc(S["g%d" % i], 1)
+        else:
+            sc.activation(T.yo[:, t:t + n], src, ActivationFunctionType.Copy).then_inc(S["g%d" % i], 1)
+        sy.wait_ge(S["g%d" % i], 1)
+        sy.dma_start(T.y[:, t:t + n], T.yo[:, t:t + n]).then_inc(S.st, 16)
+        t += n
+    sy.wait_ge(S.st, 16 * len(PIECES))
+    g.wait_ge(S.ls, nls)

@@ -6,9 +6,10 @@ J, Q = 1024, 8192
 PITCH = 12
 NB = 65
 SGP = 72
-BATCH = 4
+BATCH = 2
 MAGIC = 1.5 * 2.0 ** 30
-PIECES = [(512, "s"), (512, "v"), (1024, "s"), (1024, "v"), (1536, "s"), (1280, "v"), (1152, "s"), (1152, "v")]
+XA = 256
+PIECES = [(512, "s"), (512, "v"), (1024, "s"), (1024, "v"), (1280, "s"), (1152, "v"), (896, "s"), (768, "v"), (576, "s"), (448, "v")]
 
 SCRATCH = {
     "lnr": ("sbuf", [128, 64], "int32"),
@@ -16,7 +17,6 @@ SCRATCH = {
     "RH": ("sbuf", [128, 20], "float32"),
     "TL": ("sbuf", [128, 128], "float32"),
     "ones": ("sbuf", [128, 72], "float32"),
-    "neg": ("sbuf", [128, 8], "float32"),
     "e127": ("sbuf", [128, 4], "float32"),
     "f127": ("sbuf", [128, 4], "float32"),
     "kc": ("sbuf", [128, 8], "float32"),
@@ -37,70 +37,60 @@ SCRATCH = {
     "win": ("sbuf", [128, 3 * J + 16], "bfloat16"),
     "yo": ("sbuf", [128, Q], "bfloat16"),
     "psD": ("psum", [128, 512], "float32"),
+    "psT": ("psum", [128, 512], "float32"),
     "psW": ("psum", [128, 512], "float32"),
     "psO": ("psum", [128, 512], "float32"),
 }
-SEMAPHORES = (["ln", "lx", "m1", "m2", "gr", "gs", "ga", "vc", "pd", "vd", "vf", "sab", "cin", "xin", "ls", "vq", "va",
+SEMAPHORES = (["ln", "lxa", "lxb", "m2", "rh", "gs", "ga", "vc", "pt", "pd", "vd", "vf", "sab", "cin", "xin", "ls", "vq", "va",
                "pw", "vw", "po", "ve0", "ve1", "st"]
-              + ["cv%d" % b for b in range(6)] + ["cs%d" % b for b in range(6)] + ["g%d" % i for i in range(len(PIECES))])
+              + ["cv%d" % b for b in range(24 // BATCH)] + ["cs%d" % b for b in range(24 // BATCH)] + ["g%d" % i for i in range(len(PIECES))])
 
 
 def engines(mask):
     return bin(mask).count("1")
 
 
-def plan(topo, src, on, off):
-    m_off = 0
-    for d in off:
-        m_off = topo.mask(src, d)
-    m_on = 0
-    for d in on:
-        m_on = topo.mask(src, d) & ~m_off
-    return m_on, m_off
+def first_half(mask):
+    bits = [i for i in range(mask.bit_length()) if (mask >> i) & 1]
+    return sum(1 << i for i in bits[:len(bits) // 2])
 
 
-def split_dsts(topo, src, dsts):
-    on = [d for d in dsts if topo.chip(d) == topo.chip(src)]
-    return on, [d for d in dsts if d not in on]
+def transfers_of(topo, cores, k, kind):
+    me = cores[k]
+    ranks = [s for s in range(len(cores)) if s != k]
+    on = [s for s in ranks if topo.chip(cores[s]) == topo.chip(me)]
+    off = [s for s in ranks if s not in on]
+    m_off = topo.mask(me, cores[off[0]])
+    m_up = topo.mask(me, cores[on[0]]) & ~m_off
+    near = [s for s in on if abs(s - k) == 1]
+    if kind == "xa":
+        out = [(near[:1], m_off)]
+    elif kind == "xb":
+        out = [(near[:1], m_up)]
+    elif kind == "xo":
+        out = [([s for s in off if abs(s - k) == 1], m_off), (near[1:], m_up)]
+    else:
+        out = [([s for s in off if s >= k - 1], m_off), ([s for s in on if s >= k - 1], first_half(m_up))]
+    return [(d, m) for d, m in out if d]
 
 
-def c_dsts(cores, r):
-    return [cores[s] for s in range(len(cores)) if s != r and s >= r - 1]
+def arrivals(topo, cores, r, kinds):
+    return sum(engines(m) for kind in kinds for k in range(len(cores)) if k != r
+               for d, m in transfers_of(topo, cores, k, kind) if r in d)
 
 
-def x_dsts(cores, r):
-    return [cores[s] for s in (r - 1, r + 1) if 0 <= s < len(cores)]
-
-
-def count_in(topo, cores, r, dsts_of):
-    tot = 0
-    for k in range(len(cores)):
-        if k == r:
-            continue
-        dsts = dsts_of(cores, k)
-        if cores[r] not in dsts:
-            continue
-        on, off = split_dsts(topo, cores[k], dsts)
-        m_on, m_off = plan(topo, cores[k], on, off)
-        tot += engines(m_on if cores[r] in on else m_off)
-    return tot
-
-
-def send(g, topo, core, dsts, outs, src, remote_sem, local_sem):
-    on, off = split_dsts(topo, core, dsts)
-    m_on, m_off = plan(topo, core, on, off)
-    transfers, n = [], 0
-    for group, m in ((off, m_off), (on, m_on)):
-        if group:
-            ids = []
-            for d in group:
-                rid, pid, _ = topo.addr(d)
-                ids.append(DstId(rid=rid, pnc=pid))
-            transfers.append(RemoteDMATransfer(dst_ids=ids, dma_engine_mask=m, remote_sem=remote_sem,
-                                               srcs=[src], dsts=[outs[d] for d in group], alu_op=0))
-            n += engines(m)
-    g.remote_dma_fused(transfers, local_sem=local_sem)
-    return n
+def send(g, topo, cores, k, kind, src, out_of, remote_sem, local_sem):
+    ts = []
+    plan = transfers_of(topo, cores, k, kind)
+    for d, m in plan:
+        ids = []
+        for s in d:
+            rid, pid, _ = topo.addr(cores[s])
+            ids.append(DstId(rid=rid, pnc=pid))
+        ts.append(RemoteDMATransfer(dst_ids=ids, dma_engine_mask=m, remote_sem=remote_sem, srcs=[src], dsts=[out_of(s) for s in d], alu_op=0))
+    if ts:
+        g.remote_dma_fused(ts, local_sem=local_sem)
+    return sum(engines(m) for d, m in plan)
 
 
 def rank_program(g, core, T, topo):
@@ -120,12 +110,16 @@ def rank_program(g, core, T, topo):
     w1 = w0 + nent + (8 if tail else 0)
 
     sy.dma_start(T.lnr[0:16, :], T.ln[:]).then_inc(S.ln, 16)
-    sc.dma_start(T.win[:, J:2 * J], T.x[:]).then_inc(S.lx, 16)
+    sc.dma_start(T.win[:, J:J + XA], T.x[:, 0:XA]).then_inc(S.lxa, 16)
+    sy.dma_start(T.win[:, J + XA:2 * J], T.x[:, XA:J]).then_inc(S.lxb, 16)
 
-    v.memset(T.ones[:], 1.0).then_inc(S.m1, 1)
-    v.memset(T.neg[:], -1.0).then_inc(S.m1, 1)
+    g.iota(T.kc[:], [[-16, 8]], 0, 1, allow_small_or_imprecise_dtypes=True).then_inc(S.gs, 1)
+    g.iota(T.rowr[:], [[0, 8], [1, 16]], 0, 0, allow_small_or_imprecise_dtypes=True).then_inc(S.gs, 1)
+    g.iota(T.arow[:], [[1, 128]], 1, 0, allow_small_or_imprecise_dtypes=True).then_inc(S.ga, 1)
+    g.iota(T.brow[:, 0:NB], [[-128, NB]], 0, 0, allow_small_or_imprecise_dtypes=True).then_inc(S.ga, 1)
+
     n2 = 0
-    for ap, val in ((T.X[0:32, :], 0.0), (T.TL[0:32, :], 0.0), (T.TL[32:48, :], 1.0),
+    for ap, val in ((T.ones[:], 1.0), (T.X[0:32, :], 0.0), (T.TL[0:32, :], 0.0), (T.TL[32:48, :], 1.0),
                     (T.RH[32:48, 0:18:9], 1.0), (T.RH[32:48, 1:8], 0.0), (T.RH[32:48, 10:17], 0.0), (T.RH[32:48, 8:18:9], -1.0),
                     (T.C[:, PITCH * r + 10:PITCH * r + 12], 0.0)):
         v.memset(ap, val).then_inc(S.m2, 1)
@@ -133,19 +127,22 @@ def rank_program(g, core, T, topo):
     if tail:
         v.memset(T.win[:, w0 + nent:w1], 0.0).then_inc(S.m2, 1)
         n2 += 1
-
-    g.wait_ge(S.m1, 2)
+    v.wait_ge(S.gs, 2)
     for h in range(2):
-        g.affine_select(T.RH[0:32, 9 * h + 1:9 * h + 8], T.ones[0:32, 0:7], [[-1, 7]], ALU.is_equal, 0.0, -8 * h - 1, 1).then_inc(S.gr, 1)
-    g.affine_select(T.RH[0:32, 0:18:9], T.neg[0:32, 0:2], [[-8, 2]], ALU.is_gt, 0.0, 0, 1).then_inc(S.gr, 1)
-    g.affine_select(T.RH[0:32, 8:18:9], T.ones[0:32, 0:2], [[-8, 2]], ALU.is_gt, 0.0, -7, 1).then_inc(S.gr, 1)
-    g.affine_select(T.e127[:, 0:1], T.ones[:, 0:1], [[0, 1]], ALU.is_equal, 0.0, -127, 1).then_inc(S.gs, 1)
-    g.iota(T.kc[:], [[-16, 8]], 0, 1, allow_small_or_imprecise_dtypes=True).then_inc(S.gs, 1)
-    g.iota(T.rowr[:], [[0, 8], [1, 16]], 0, 0, allow_small_or_imprecise_dtypes=True).then_inc(S.gs, 1)
-    g.iota(T.arow[:], [[1, 128]], 1, 0, allow_small_or_imprecise_dtypes=True).then_inc(S.ga, 1)
-    g.iota(T.brow[:, 0:NB], [[-128, NB]], 0, 0, allow_small_or_imprecise_dtypes=True).then_inc(S.ga, 1)
+        a, b = 9 * h, 8 * h
+        q = T.kc[0:32, 0:1]
+        v.tensor_scalar(T.RH[0:32, a + 1:a + 8], T.rowr[0:32, b + 1:b + 8], q, None, ALU.is_equal).then_inc(S.rh, 1)
+        v.tensor_scalar(T.RH[0:32, a:a + 1], T.rowr[0:32, b:b + 1], q, -1.0, ALU.is_lt, ALU.mult).then_inc(S.rh, 1)
+        v.tensor_scalar(T.RH[0:32, a + 8:a + 9], T.rowr[0:32, b + 7:b + 8], q, None, ALU.is_lt).then_inc(S.rh, 1)
+    v.tensor_scalar(T.e127[:, 0:1], T.kc[:, 0:1], 127.0, None, ALU.is_equal).then_inc(S.vf, 1)
+    v.tensor_scalar(T.f127[:, 0:1], T.kc[:, 0:1], 127.0, 1.0, ALU.is_equal, ALU.subtract).then_inc(S.vf, 1)
 
-    v.wait_ge(S.m1, 2)
+    def slot_x(s):
+        return J * (r - s + 1)
+    nls = 0
+    g.wait_ge(S.lxa, 16)
+    nls += send(g, topo, cores, r, "xa", T.win[:, J:J + XA], lambda s: T.win[:, slot_x(s):slot_x(s) + XA], S.xin, S.ls)
+
     v.wait_ge(S.m2, n2)
     v.wait_ge(S.ln, 16)
     v.tensor_copy(T.X[0:16, :], T.lnr[0:16, :]).then_inc(S.vc, 1)
@@ -153,32 +150,27 @@ def rank_program(g, core, T, topo):
     v.tensor_tensor_scan(T.X[32:48, :], T.ones[0:16, 0:64], T.X[0:16, :], 0.0, ALU.mult, ALU.add).then_inc(S.vc, 1)
 
     te.wait_ge(S.m2, n2)
-    te.wait_ge(S.gr, 4)
+    te.wait_ge(S.rh, 6)
     te.wait_ge(S.vc, 2)
+    te.matmul(T.psT[:, 0:1], T.TL[0:48, :], T.X[0:48, 63:64], True, True).then_inc(S.pt, 1)
+    te.matmul(T.psD[0:64, 0:18], T.X[0:48, :], T.RH[0:48, 0:18], True, True).then_inc(S.pd, 1)
+
+    c = PITCH * r
+    v.wait_ge(S.pt, 1)
+    v.tensor_copy(T.C[:, c + 9:c + 10], T.psT[:, 0:1]).then_inc(S.vd, 1)
+    v.wait_ge(S.pd, 1)
     for h in range(2):
-        te.matmul(T.psD[64 * h:64 * h + 64, 0:9], T.X[0:48, :], T.RH[0:48, 9 * h:9 * h + 9], True, True).then_inc(S.pd, 1)
-    te.matmul(T.psD[:, 9:10], T.TL[0:48, :], T.X[0:48, 63:64], True, True).then_inc(S.pd, 1)
+        v.tensor_copy(T.C[64 * h:64 * h + 64, c:c + 9], T.psD[0:64, 9 * h:9 * h + 9]).then_inc(S.vd, 1)
 
-    v.wait_ge(S.pd, 3)
-    v.tensor_copy(T.C[:, PITCH * r:PITCH * r + 10], T.psD[:, 0:10]).then_inc(S.vd, 1)
-
-    nls = 0
+    slot = T.C[:, c:c + PITCH]
     g.wait_ge(S.m2, n2)
-    g.wait_ge(S.vd, 1)
-    dsts = c_dsts(cores, r)
-    slot = T.C[:, PITCH * r:PITCH * r + PITCH]
-    nls += send(g, topo, core, dsts, {d: slot for d in dsts}, slot, S.cin, S.ls)
-    g.wait_ge(S.lx, 16)
-    dsts = x_dsts(cores, r)
-    outs = {}
-    for d in dsts:
-        a = J * (r - T.rank_of(d) + 1)
-        outs[d] = T.win[:, a:a + J]
-    nls += send(g, topo, core, dsts, outs, T.win[:, J:2 * J], S.xin, S.ls)
+    g.wait_ge(S.vd, 3)
+    nls += send(g, topo, cores, r, "c", slot, lambda s: slot, S.cin, S.ls)
+    g.wait_ge(S.lxb, 16)
+    nls += send(g, topo, cores, r, "xo", T.win[:, J:2 * J], lambda s: T.win[:, slot_x(s):slot_x(s) + J], S.xin, S.ls)
+    nls += send(g, topo, cores, r, "xb", T.win[:, J + XA:2 * J], lambda s: T.win[:, slot_x(s) + XA:slot_x(s) + J], S.xin, S.ls)
 
-    v.wait_ge(S.gs, 3)
-    v.tensor_scalar(T.f127[:, 0:1], T.e127[:, 0:1], 1.0, None, ALU.subtract).then_inc(S.vf, 1)
-    v.wait_ge(S.vf, 1)
+    v.wait_ge(S.vf, 2)
     for h in range(8):
         v.tensor_scalar(T.SA[:, 128 * h:128 * h + 128], T.rowr[:], T.kc[:, h:h + 1], T.e127[:, 0:1], ALU.is_equal, ALU.add).then_inc(S.sab, 1)
         v.tensor_scalar(T.SB[:, 128 * h:128 * h + 128], T.rowr[:], T.kc[:, h:h + 1], T.f127[:, 0:1], ALU.not_equal, ALU.add).then_inc(S.sab, 1)
@@ -186,8 +178,9 @@ def rank_program(g, core, T, topo):
     ncol = PITCH * (hi + 1)
     c0 = PITCH * lo
     cw = ncol - c0
-    v.wait_ge(S.vd, 1)
-    v.wait_ge(S.cin, count_in(topo, cores, r, c_dsts))
+    v.wait_ge(S.vd, 3)
+    v.wait_ge(S.ga, 2)
+    v.wait_ge(S.cin, arrivals(topo, cores, r, ["c"]))
     v.tensor_tensor_scan(T.Cc[:, 0:ncol], T.ones[:, 0:ncol], T.C[:, 0:ncol], 0.5 - Q * r, ALU.mult, ALU.add).then_inc(S.vq, 1)
     v.wait_ge(S.vq, 1)
     v.tensor_scalar(T.M[:, 0:cw], T.Cc[:, c0:ncol], -64.0, MAGIC, ALU.add, ALU.add).then_inc(S.va, 1)
@@ -196,7 +189,6 @@ def rank_program(g, core, T, topo):
     v.wait_ge(S.va, 2)
     v.tensor_tensor(T.A[:, 0:cw], T.Cc[:, c0:ncol], T.FB[:, 0:cw], ALU.subtract).then_inc(S.va, 1)
     v.wait_ge(S.va, 3)
-    v.wait_ge(S.ga, 2)
     col = [PITCH * (k // 8) + k % 8 for k in range(nch)]
     for k in range(nch):
         v.tensor_scalar(T.LE[:, 128 * k:128 * k + 128], T.arow[:], T.A[:, col[k]:col[k] + 1], 0.5, ALU.is_ge, ALU.subtract).then_inc(S["cv%d" % (k // BATCH)], 1)
@@ -207,8 +199,8 @@ def rank_program(g, core, T, topo):
                       bias=T.Cc[:, c0 + col[k]:c0 + col[k] + 1]).then_inc(S["cs%d" % (k // BATCH)], 1)
     for k in range(nch):
         if k % BATCH == 0:
-            te.wait_ge(S["cv%d" % (k // BATCH)], BATCH)
             te.wait_ge(S["cs%d" % (k // BATCH)], BATCH)
+            te.wait_ge(S["cv%d" % (k // BATCH)], BATCH)
         mm = te.matmul(T.psW[:, 0:NB], T.LE[:, 128 * k:128 * k + 128], T.SG[:, SGP * k:SGP * k + NB], k == 0, k == nch - 1)
         if k == nch - 1:
             mm.then_inc(S.pw, 1)
@@ -225,10 +217,11 @@ def rank_program(g, core, T, topo):
     v.tensor_scalar(T.off[:, 0:e0], T.psO[:, 0:e0], -0.5, nent / 2.0, ALU.mult, ALU.add).then_inc(S.ve0, 1)
     v.tensor_scalar(T.off[:, e0:512], T.psO[:, e0:512], -0.5, nent / 2.0, ALU.mult, ALU.add).then_inc(S.ve1, 1)
 
-    nx = count_in(topo, cores, r, x_dsts)
+    nx = arrivals(topo, cores, r, ["xa", "xb", "xo"])
     for q in (v, sc):
         q.wait_ge(S.xin, nx)
-        q.wait_ge(S.lx, 16)
+        q.wait_ge(S.lxa, 16)
+        q.wait_ge(S.lxb, 16)
         q.wait_ge(S.ve0, 1)
     sc.wait_ge(S.m2, n2)
     waited = {"s": False, "v": False}

@@ -7,7 +7,7 @@ PITCH = 12
 NB = 65
 SGP = 72
 BATCH = 2
-MAGIC = 1.5 * 2.0 ** 30
+UNIT = 1.0 / 128
 XA = 256
 PIECES = [(512, "s"), (512, "v"), (1024, "s"), (1024, "v"), (1280, "s"), (1152, "v"), (896, "s"), (768, "v"), (576, "s"), (448, "v")]
 
@@ -22,14 +22,14 @@ SCRATCH = {
     "kc": ("sbuf", [128, 8], "float32"),
     "rowr": ("sbuf", [128, 128], "bfloat16"),
     "arow": ("sbuf", [128, 128], "bfloat16"),
+    "aunit": ("sbuf", [128, 128], "bfloat16"),
     "brow": ("sbuf", [128, SGP], "bfloat16"),
     "SA": ("sbuf", [128, 1024], "bfloat16"),
     "SB": ("sbuf", [128, 1024], "bfloat16"),
     "C": ("sbuf", [128, 72], "float32"),
     "Cc": ("sbuf", [128, 72], "float32"),
-    "M": ("sbuf", [128, 36], "float32"),
-    "FB": ("sbuf", [128, 36], "float32"),
-    "A": ("sbuf", [128, 36], "float32"),
+    "B": ("sbuf", [128, 36], "int32"),
+    "A": ("sbuf", [128, 40], "bfloat16"),
     "LE": ("sbuf", [128, 24 * 128], "bfloat16"),
     "SG": ("sbuf", [128, 24 * SGP], "bfloat16"),
     "W16": ("sbuf", [128, SGP], "float16"),
@@ -115,12 +115,12 @@ def rank_program(g, core, T, topo):
 
     g.iota(T.kc[:], [[-16, 8]], 0, 1, allow_small_or_imprecise_dtypes=True).then_inc(S.gs, 1)
     g.iota(T.rowr[:], [[0, 8], [1, 16]], 0, 0, allow_small_or_imprecise_dtypes=True).then_inc(S.gs, 1)
-    g.iota(T.arow[:], [[1, 128]], 1, 0, allow_small_or_imprecise_dtypes=True).then_inc(S.ga, 1)
-    g.iota(T.brow[:, 0:NB], [[-128, NB]], 0, 0, allow_small_or_imprecise_dtypes=True).then_inc(S.ga, 1)
+    g.iota(T.arow[:], [[1, 128]], -63, 0, allow_small_or_imprecise_dtypes=True).then_inc(S.ga, 1)
+    g.iota(T.brow[:, 0:NB], [[-2, NB]], 1, 0, allow_small_or_imprecise_dtypes=True).then_inc(S.ga, 1)
 
     n2 = 0
-    for ap, val in ((T.ones[:], 1.0), (T.X[0:32, :], 0.0), (T.TL[0:32, :], 0.0), (T.TL[32:48, :], 1.0),
-                    (T.RH[32:48, 0:18:9], 1.0), (T.RH[32:48, 1:8], 0.0), (T.RH[32:48, 10:17], 0.0), (T.RH[32:48, 8:18:9], -1.0),
+    for ap, val in ((T.ones[:], 1.0), (T.X[0:32, :], 0.0), (T.TL[0:32, :], 0.0), (T.TL[32:48, :], UNIT),
+                    (T.RH[32:48, 0:18:9], UNIT), (T.RH[32:48, 1:8], 0.0), (T.RH[32:48, 10:17], 0.0), (T.RH[32:48, 8:18:9], -UNIT),
                     (T.C[:, PITCH * r + 10:PITCH * r + 12], 0.0)):
         v.memset(ap, val).then_inc(S.m2, 1)
         n2 += 1
@@ -131,9 +131,9 @@ def rank_program(g, core, T, topo):
     for h in range(2):
         a, b = 9 * h, 8 * h
         q = T.kc[0:32, 0:1]
-        v.tensor_scalar(T.RH[0:32, a + 1:a + 8], T.rowr[0:32, b + 1:b + 8], q, None, ALU.is_equal).then_inc(S.rh, 1)
-        v.tensor_scalar(T.RH[0:32, a:a + 1], T.rowr[0:32, b:b + 1], q, -1.0, ALU.is_lt, ALU.mult).then_inc(S.rh, 1)
-        v.tensor_scalar(T.RH[0:32, a + 8:a + 9], T.rowr[0:32, b + 7:b + 8], q, None, ALU.is_lt).then_inc(S.rh, 1)
+        v.tensor_scalar(T.RH[0:32, a + 1:a + 8], T.rowr[0:32, b + 1:b + 8], q, UNIT, ALU.is_equal, ALU.mult).then_inc(S.rh, 1)
+        v.tensor_scalar(T.RH[0:32, a:a + 1], T.rowr[0:32, b:b + 1], q, -UNIT, ALU.is_lt, ALU.mult).then_inc(S.rh, 1)
+        v.tensor_scalar(T.RH[0:32, a + 8:a + 9], T.rowr[0:32, b + 7:b + 8], q, UNIT, ALU.is_lt, ALU.mult).then_inc(S.rh, 1)
     v.tensor_scalar(T.e127[:, 0:1], T.kc[:, 0:1], 127.0, None, ALU.is_equal).then_inc(S.vf, 1)
     v.tensor_scalar(T.f127[:, 0:1], T.kc[:, 0:1], 127.0, 1.0, ALU.is_equal, ALU.subtract).then_inc(S.vf, 1)
 
@@ -152,15 +152,15 @@ def rank_program(g, core, T, topo):
     te.wait_ge(S.m2, n2)
     te.wait_ge(S.rh, 6)
     te.wait_ge(S.vc, 2)
-    te.matmul(T.psT[:, 0:1], T.TL[0:48, :], T.X[0:48, 63:64], True, True).then_inc(S.pt, 1)
     te.matmul(T.psD[0:64, 0:18], T.X[0:48, :], T.RH[0:48, 0:18], True, True).then_inc(S.pd, 1)
+    te.matmul(T.psT[:, 0:1], T.TL[0:48, :], T.X[0:48, 63:64], True, True).then_inc(S.pt, 1)
 
     c = PITCH * r
-    v.wait_ge(S.pt, 1)
-    v.tensor_copy(T.C[:, c + 9:c + 10], T.psT[:, 0:1]).then_inc(S.vd, 1)
     v.wait_ge(S.pd, 1)
     for h in range(2):
         v.tensor_copy(T.C[64 * h:64 * h + 64, c:c + 9], T.psD[0:64, 9 * h:9 * h + 9]).then_inc(S.vd, 1)
+    v.wait_ge(S.pt, 1)
+    v.tensor_copy(T.C[:, c + 9:c + 10], T.psT[:, 0:1]).then_inc(S.vd, 1)
 
     slot = T.C[:, c:c + PITCH]
     g.wait_ge(S.m2, n2)
@@ -171,6 +171,8 @@ def rank_program(g, core, T, topo):
     nls += send(g, topo, cores, r, "xb", T.win[:, J + XA:2 * J], lambda s: T.win[:, slot_x(s) + XA:slot_x(s) + J], S.xin, S.ls)
 
     v.wait_ge(S.vf, 2)
+    v.wait_ge(S.ga, 2)
+    v.tensor_scalar(T.aunit[:], T.arow[:], UNIT, None, ALU.mult).then_inc(S.vf, 1)
     for h in range(8):
         v.tensor_scalar(T.SA[:, 128 * h:128 * h + 128], T.rowr[:], T.kc[:, h:h + 1], T.e127[:, 0:1], ALU.is_equal, ALU.add).then_inc(S.sab, 1)
         v.tensor_scalar(T.SB[:, 128 * h:128 * h + 128], T.rowr[:], T.kc[:, h:h + 1], T.f127[:, 0:1], ALU.not_equal, ALU.add).then_inc(S.sab, 1)
@@ -179,24 +181,22 @@ def rank_program(g, core, T, topo):
     c0 = PITCH * lo
     cw = ncol - c0
     v.wait_ge(S.vd, 3)
-    v.wait_ge(S.ga, 2)
+    v.wait_ge(S.vf, 3)
     v.wait_ge(S.cin, arrivals(topo, cores, r, ["c"]))
-    v.tensor_tensor_scan(T.Cc[:, 0:ncol], T.ones[:, 0:ncol], T.C[:, 0:ncol], 0.5 - Q * r, ALU.mult, ALU.add).then_inc(S.vq, 1)
+    v.tensor_tensor_scan(T.Cc[:, 0:ncol], T.ones[:, 0:ncol], T.C[:, 0:ncol], (-Q * r - 63.5) * UNIT, ALU.mult, ALU.add).then_inc(S.vq, 1)
     v.wait_ge(S.vq, 1)
-    v.tensor_scalar(T.M[:, 0:cw], T.Cc[:, c0:ncol], -64.0, MAGIC, ALU.add, ALU.add).then_inc(S.va, 1)
+    v.tensor_copy(T.B[:, 0:cw], T.Cc[:, c0:ncol]).then_inc(S.va, 1)
     v.wait_ge(S.va, 1)
-    v.tensor_scalar(T.FB[:, 0:cw], T.M[:, 0:cw], MAGIC, None, ALU.subtract).then_inc(S.va, 1)
+    v.tensor_tensor(T.A[:, 0:cw], T.Cc[:, c0:ncol], T.B[:, 0:cw], ALU.subtract).then_inc(S.va, 1)
     v.wait_ge(S.va, 2)
-    v.tensor_tensor(T.A[:, 0:cw], T.Cc[:, c0:ncol], T.FB[:, 0:cw], ALU.subtract).then_inc(S.va, 1)
-    v.wait_ge(S.va, 3)
     col = [PITCH * (k // 8) + k % 8 for k in range(nch)]
     for k in range(nch):
-        v.tensor_scalar(T.LE[:, 128 * k:128 * k + 128], T.arow[:], T.A[:, col[k]:col[k] + 1], 0.5, ALU.is_ge, ALU.subtract).then_inc(S["cv%d" % (k // BATCH)], 1)
+        v.tensor_scalar(T.LE[:, 128 * k:128 * k + 128], T.aunit[:], T.A[:, col[k]:col[k] + 1], 0.5, ALU.is_ge, ALU.subtract).then_inc(S["cv%d" % (k // BATCH)], 1)
     sc.wait_ge(S.ga, 2)
     sc.wait_ge(S.vq, 1)
     for k in range(nch):
         sc.activation(T.SG[:, SGP * k:SGP * k + NB], T.brow[:, 0:NB], ActivationFunctionType.Sign,
-                      bias=T.Cc[:, c0 + col[k]:c0 + col[k] + 1]).then_inc(S["cs%d" % (k // BATCH)], 1)
+                      bias=T.Cc[:, c0 + col[k]:c0 + col[k] + 1], scale=0.5).then_inc(S["cs%d" % (k // BATCH)], 1)
     for k in range(nch):
         if k % BATCH == 0:
             te.wait_ge(S["cs%d" % (k // BATCH)], BATCH)

from concourse.bass import DstId, RemoteDMATransfer
from concourse.mybir import AluOpType, ActivationFunctionType

ALU = AluOpType
J, Q = 1024, 8192
PITCH = 12
NB = 65
SGP = 72
BATCH = 2
UNIT = 1.0 / 128
XA = 256
PIECES = [(512, "s"), (512, "v"), (1024, "s"), (1024, "v"), (1280, "s"), (1152, "v"), (896, "s"), (768, "v"), (576, "s"), (448, "v")]

SCRATCH = {
    "lnr": ("sbuf", [128, 64], "int32"),
    "X": ("sbuf", [128, 64], "float32"),
    "RH": ("sbuf", [128, 20], "float32"),
    "TL": ("sbuf", [128, 128], "float32"),
    "ones": ("sbuf", [128, 72], "float32"),
    "e127": ("sbuf", [128, 4], "float32"),
    "f127": ("sbuf", [128, 4], "float32"),
    "kc": ("sbuf", [128, 8], "float32"),
    "rowr": ("sbuf", [128, 128], "bfloat16"),
    "arow": ("sbuf", [128, 128], "bfloat16"),
    "aunit": ("sbuf", [128, 128], "bfloat16"),
    "brow": ("sbuf", [128, SGP], "bfloat16"),
    "SA": ("sbuf", [128, 1024], "bfloat16"),
    "SB": ("sbuf", [128, 1024], "bfloat16"),
    "C": ("sbuf", [128, 72], "float32"),
    "Cc": ("sbuf", [128, 72], "float32"),
    "B": ("sbuf", [128, 36], "int32"),
    "A": ("sbuf", [128, 40], "bfloat16"),
    "LE": ("sbuf", [128, 24 * 128], "bfloat16"),
    "SG": ("sbuf", [128, 24 * SGP], "bfloat16"),
    "W16": ("sbuf", [128, SGP], "float16"),
    "off": ("sbuf", [128, 512], "uint16"),
    "win": ("sbuf", [128, 3 * J + 16], "bfloat16"),
    "yo": ("sbuf", [128, Q], "bfloat16"),
    "psD": ("psum", [128, 512], "float32"),
    "psT": ("psum", [128, 512], "float32"),
    "psW": ("psum", [128, 512], "float32"),
    "psO": ("psum", [128, 512], "float32"),
}
SEMAPHORES = (["ln", "lxa", "lxb", "m2", "rh", "gs", "ga", "vc", "pt", "pd", "vd", "vf", "sab", "cin", "xin", "ls", "vq", "va",
               "pw", "vw", "po", "ve0", "ve1", "st"]
              + ["cv%d" % b for b in range(24 // BATCH)] + ["cs%d" % b for b in range(24 // BATCH)] + ["g%d" % i for i in range(len(PIECES))])


def engines(mask):
    return bin(mask).count("1")


def first_half(mask):
    bits = [i for i in range(mask.bit_length()) if (mask >> i) & 1]
    return sum(1 << i for i in bits[:len(bits) // 2])


def transfers_of(topo, cores, k, kind):
    me = cores[k]
    ranks = [s for s in range(len(cores)) if s != k]
    on = [s for s in ranks if topo.chip(cores[s]) == topo.chip(me)]
    off = [s for s in ranks if s not in on]
    m_off = topo.mask(me, cores[off[0]])
    m_up = topo.mask(me, cores[on[0]]) & ~m_off
    near = [s for s in on if abs(s - k) == 1]
    if kind == "xa":
        out = [(near[:1], m_off)]
    elif kind == "xb":
        out = [(near[:1], m_up)]
    elif kind == "xo":
        out = [([s for s in off if abs(s - k) == 1], m_off), (near[1:], m_up)]
    else:
        out = [([s for s in off if s >= k - 1], m_off), ([s for s in on if s >= k - 1], first_half(m_up))]
    return [(d, m) for d, m in out if d]


def arrivals(topo, cores, r, kinds):
    return sum(engines(m) for kind in kinds for k in range(len(cores)) if k != r
               for d, m in transfers_of(topo, cores, k, kind) if r in d)


def send(g, topo, cores, k, kind, src, out_of, remote_sem, local_sem):
    ts = []
    plan = transfers_of(topo, cores, k, kind)
    for d, m in plan:
        ids = []
        for s in d:
            rid, pid, _ = topo.addr(cores[s])
            ids.append(DstId(rid=rid, pnc=pid))
        ts.append(RemoteDMATransfer(dst_ids=ids, dma_engine_mask=m, remote_sem=remote_sem, srcs=[src], dsts=[out_of(s) for s in d], alu_op=0))
    if ts:
        g.remote_dma_fused(ts, local_sem=local_sem)
    return sum(engines(m) for d, m in plan)


def rank_program(g, core, T, topo):
    r = T.rank_of(core)
    if r is None:
        return
    cores = T.cores
    n_ranks = len(cores)
    lo, hi = max(r - 1, 0), min(r + 1, n_ranks - 1)
    nl = hi - lo + 1
    nent = nl * J
    nch = nl * 8
    S = T.sem
    v, sc, sy, te = g.vector, g.scalar, g.sync, g.tensor
    w0 = J * (lo - (r - 1))
    tail = r >= n_ranks - 2
    w1 = w0 + nent + (8 if tail else 0)

    sy.dma_start(T.lnr[0:16, :], T.ln[:]).then_inc(S.ln, 16)
    sc.dma_start(T.win[:, J:J + XA], T.x[:, 0:XA]).then_inc(S.lxa, 16)
    sy.dma_start(T.win[:, J + XA:2 * J], T.x[:, XA:J]).then_inc(S.lxb, 16)

    g.iota(T.kc[:], [[-16, 8]], 0, 1, allow_small_or_imprecise_dtypes=True).then_inc(S.gs, 1)
    g.iota(T.rowr[:], [[0, 8], [1, 16]], 0, 0, allow_small_or_imprecise_dtypes=True).then_inc(S.gs, 1)
    g.iota(T.arow[:], [[1, 128]], -63, 0, allow_small_or_imprecise_dtypes=True).then_inc(S.ga, 1)
    g.iota(T.brow[:, 0:NB], [[-2, NB]], 1, 0, allow_small_or_imprecise_dtypes=True).then_inc(S.ga, 1)

    n2 = 0
    for ap, val in ((T.ones[:], 1.0), (T.X[0:32, :], 0.0), (T.TL[0:32, :], 0.0), (T.TL[32:48, :], UNIT),
                    (T.RH[32:48, 0:18:9], UNIT), (T.RH[32:48, 1:8], 0.0), (T.RH[32:48, 10:17], 0.0), (T.RH[32:48, 8:18:9], -UNIT),
                    (T.C[:, PITCH * r + 10:PITCH * r + 12], 0.0)):
        v.memset(ap, val).then_inc(S.m2, 1)
        n2 += 1
    if tail:
        v.memset(T.win[:, w0 + nent:w1], 0.0).then_inc(S.m2, 1)
        n2 += 1
    v.wait_ge(S.gs, 2)
    for h in range(2):
        a, b = 9 * h, 8 * h
        q = T.kc[0:32, 0:1]
        v.tensor_scalar(T.RH[0:32, a + 1:a + 8], T.rowr[0:32, b + 1:b + 8], q, UNIT, ALU.is_equal, ALU.mult).then_inc(S.rh, 1)
        v.tensor_scalar(T.RH[0:32, a:a + 1], T.rowr[0:32, b:b + 1], q, -UNIT, ALU.is_lt, ALU.mult).then_inc(S.rh, 1)
        v.tensor_scalar(T.RH[0:32, a + 8:a + 9], T.rowr[0:32, b + 7:b + 8], q, UNIT, ALU.is_lt, ALU.mult).then_inc(S.rh, 1)
    v.tensor_scalar(T.e127[:, 0:1], T.kc[:, 0:1], 127.0, None, ALU.is_equal).then_inc(S.vf, 1)
    v.tensor_scalar(T.f127[:, 0:1], T.kc[:, 0:1], 127.0, 1.0, ALU.is_equal, ALU.subtract).then_inc(S.vf, 1)

    def slot_x(s):
        return J * (r - s + 1)
    nls = 0
    g.wait_ge(S.lxa, 16)
    nls += send(g, topo, cores, r, "xa", T.win[:, J:J + XA], lambda s: T.win[:, slot_x(s):slot_x(s) + XA], S.xin, S.ls)

    v.wait_ge(S.m2, n2)
    v.wait_ge(S.ln, 16)
    v.tensor_copy(T.X[0:16, :], T.lnr[0:16, :]).then_inc(S.vc, 1)
    v.wait_ge(S.vc, 1)
    v.tensor_tensor_scan(T.X[32:48, :], T.ones[0:16, 0:64], T.X[0:16, :], 0.0, ALU.mult, ALU.add).then_inc(S.vc, 1)

    te.wait_ge(S.m2, n2)
    te.wait_ge(S.rh, 6)
    te.wait_ge(S.vc, 2)
    te.matmul(T.psD[0:64, 0:18], T.X[0:48, :], T.RH[0:48, 0:18], True, True).then_inc(S.pd, 1)
    te.matmul(T.psT[:, 0:1], T.TL[0:48, :], T.X[0:48, 63:64], True, True).then_inc(S.pt, 1)

    c = PITCH * r
    v.wait_ge(S.pd, 1)
    for h in range(2):
        v.tensor_copy(T.C[64 * h:64 * h + 64, c:c + 9], T.psD[0:64, 9 * h:9 * h + 9]).then_inc(S.vd, 1)
    v.wait_ge(S.pt, 1)
    v.tensor_copy(T.C[:, c + 9:c + 10], T.psT[:, 0:1]).then_inc(S.vd, 1)

    slot = T.C[:, c:c + PITCH]
    g.wait_ge(S.m2, n2)
    g.wait_ge(S.vd, 3)
    nls += send(g, topo, cores, r, "c", slot, lambda s: slot, S.cin, S.ls)
    g.wait_ge(S.lxb, 16)
    nls += send(g, topo, cores, r, "xo", T.win[:, J:2 * J], lambda s: T.win[:, slot_x(s):slot_x(s) + J], S.xin, S.ls)
    nls += send(g, topo, cores, r, "xb", T.win[:, J + XA:2 * J], lambda s: T.win[:, slot_x(s) + XA:slot_x(s) + J], S.xin, S.ls)

    v.wait_ge(S.vf, 2)
    v.wait_ge(S.ga, 2)
    v.tensor_scalar(T.aunit[:], T.arow[:], UNIT, None, ALU.mult).then_inc(S.vf, 1)
    for h in range(8):
        v.tensor_scalar(T.SA[:, 128 * h:128 * h + 128], T.rowr[:], T.kc[:, h:h + 1], T.e127[:, 0:1], ALU.is_equal, ALU.add).then_inc(S.sab, 1)
        v.tensor_scalar(T.SB[:, 128 * h:128 * h + 128], T.rowr[:], T.kc[:, h:h + 1], T.f127[:, 0:1], ALU.not_equal, ALU.add).then_inc(S.sab, 1)

    ncol = PITCH * (hi + 1)
    c0 = PITCH * lo
    cw = ncol - c0
    v.wait_ge(S.vd, 3)
    v.wait_ge(S.vf, 3)
    v.wait_ge(S.cin, arrivals(topo, cores, r, ["c"]))
    v.tensor_tensor_scan(T.Cc[:, 0:ncol], T.ones[:, 0:ncol], T.C[:, 0:ncol], (-Q * r - 63.5) * UNIT, ALU.mult, ALU.add).then_inc(S.vq, 1)
    v.wait_ge(S.vq, 1)
    v.tensor_copy(T.B[:, 0:cw], T.Cc[:, c0:ncol]).then_inc(S.va, 1)
    v.wait_ge(S.va, 1)
    v.tensor_tensor(T.A[:, 0:cw], T.Cc[:, c0:ncol], T.B[:, 0:cw], ALU.subtract).then_inc(S.va, 1)
    v.wait_ge(S.va, 2)
    col = [PITCH * (k // 8) + k % 8 for k in range(nch)]
    for k in range(nch):
        v.tensor_scalar(T.LE[:, 128 * k:128 * k + 128], T.aunit[:], T.A[:, col[k]:col[k] + 1], 0.5, ALU.is_ge, ALU.subtract).then_inc(S["cv%d" % (k // BATCH)], 1)
    sc.wait_ge(S.ga, 2)
    sc.wait_ge(S.vq, 1)
    for k in range(nch):
        sc.activation(T.SG[:, SGP * k:SGP * k + NB], T.brow[:, 0:NB], ActivationFunctionType.Sign,
                      bias=T.Cc[:, c0 + col[k]:c0 + col[k] + 1], scale=0.5).then_inc(S["cs%d" % (k // BATCH)], 1)
    for k in range(nch):
        if k % BATCH == 0:
            te.wait_ge(S["cs%d" % (k // BATCH)], BATCH)
            te.wait_ge(S["cv%d" % (k // BATCH)], BATCH)
        mm = te.matmul(T.psW[:, 0:NB], T.LE[:, 128 * k:128 * k + 128], T.SG[:, SGP * k:SGP * k + NB], k == 0, k == nch - 1)
        if k == nch - 1:
            mm.then_inc(S.pw, 1)

    v.wait_ge(S.pw, 1)
    v.tensor_copy(T.W16[:, 0:NB], T.psW[:, 0:NB]).then_inc(S.vw, 1)
    te.wait_ge(S.sab, 16)
    te.wait_ge(S.vw, 1)
    for h in range(8):
        te.matmul(T.psO[:, h:512:8], T.SA[:, 128 * h:128 * h + 128], T.W16[:, 1:NB], True, False)
        te.matmul(T.psO[:, h:512:8], T.SB[:, 128 * h:128 * h + 128], T.W16[:, 0:NB - 1], False, True).then_inc(S.po, 1)
    v.wait_ge(S.po, 8)
    e0 = (PIECES[0][0] + PIECES[1][0]) // 16
    v.tensor_scalar(T.off[:, 0:e0], T.psO[:, 0:e0], -0.5, nent / 2.0, ALU.mult, ALU.add).then_inc(S.ve0, 1)
    v.tensor_scalar(T.off[:, e0:512], T.psO[:, e0:512], -0.5, nent / 2.0, ALU.mult, ALU.add).then_inc(S.ve1, 1)

    nx = arrivals(topo, cores, r, ["xa", "xb", "xo"])
    for q in (v, sc):
        q.wait_ge(S.xin, nx)
        q.wait_ge(S.lxa, 16)
        q.wait_ge(S.lxb, 16)
        q.wait_ge(S.ve0, 1)
    sc.wait_ge(S.m2, n2)
    waited = {"s": False, "v": False}
    t = 0
    for i, (n, who) in enumerate(PIECES):
        if (t + n) // 16 > e0 and not waited[who]:
            (v if who == "v" else sc).wait_ge(S.ve1, 1)
            waited[who] = True
        src = T.win[:, w0:w1].indirect(T.off[:, t // 16:(t + n) // 16])
        if who == "v":
            v.tensor_copy(T.yo[:, t:t + n], src).then_inc(S["g%d" % i], 1)
        else:
            sc.activation(T.yo[:, t:t + n], src, ActivationFunctionType.Copy).then_inc(S["g%d" % i], 1)
        sy.wait_ge(S["g%d" % i], 1)
        sy.dma_start(T.y[:, t:t + n], T.yo[:, t:t + n]).then_inc(S.st, 16)
        t += n
    sy.wait_ge(S.st, 16 * len(PIECES))
    g.wait_ge(S.ls, nls)
